import numpy as np
import ml_dtypes


def mxq(x, axis, fmt="e4m3"):
    dtype, down = {"e4m3": (ml_dtypes.float8_e4m3fn, 7), "e5m2": (ml_dtypes.float8_e5m2, 14)}[fmt]
    v = np.moveaxis(np.asarray(x, np.float32).astype(ml_dtypes.bfloat16).astype(np.float64), axis, -1)
    blocks = v.reshape(v.shape[:-1] + (-1, 32))
    amax = np.abs(blocks).max(-1, keepdims=True)
    byte = np.maximum(np.where(amax > 0, np.frexp(amax)[1] - 1 + 127, 0) - down, 1)
    scale = np.exp2(byte - 127.0)
    codes = (blocks / scale).astype(np.float32).astype(dtype).astype(np.float64)
    return np.moveaxis((codes * scale).reshape(v.shape), -1, axis)


WIDE = False


def mx_kscale(k):
    if not WIDE:
        return np.ones(k)
    levels = np.array([10, -10, 5, -5, 0])
    if k % 512:
        return np.exp2(np.random.permutation(np.resize(levels, k // 32))).repeat(32)
    a = np.empty((k // 512, 16))
    for p in range(k // 512):
        a[p, :8] = np.random.permutation(np.resize(levels, 8))
        for g in range(8):
            far = levels[np.abs(levels - a[p, g]) >= 10]
            a[p, g + 8] = far[np.random.randint(len(far))]
    return np.exp2(a.ravel()).repeat(32)


def f64(x):
    return np.asarray(x).astype(np.float64)


def striped(idx):
    return np.tile(idx.reshape(-1, 16).T, (8, 1)).astype(np.uint16)


def unstriped(offs):
    return offs[:16].T.reshape(-1).astype(np.int64)


K, T, D, S, V, H, N = 1024, 1024, 3, 512, 256, 1024, 128
P = 2 ** 7


def setup_inputs():
    n = np.random.standard_normal
    s = mx_kscale(K)[:, None]
    u = mx_kscale(H)
    q = np.random.permutation(S)
    return {
        "xT": (n((K, T)) * s).astype(np.float32),
        "w1": (n((K, H)) / np.sqrt(K) / s * u).astype(np.float32),
        "w2": (n((H, N)) / np.sqrt(H) / u[:, None]).astype(np.float32),
        "gate": np.tile(np.random.uniform(0.2, 1.0, (D, 1, V)) / np.sqrt(D), (1, P, 1)).astype(np.float32),
        "offs": striped(np.random.permutation(T)[:S]),
        "pos1": striped(q[:V]),
        "pos2": striped(q[V:]),
        "pos3": striped(np.random.permutation(S)[:V]),
    }


def reference(xT, w1, w2, gate, offs, pos1, pos2, pos3):
    h = mxq(f64(w1), 0, "e4m3").T @ mxq(f64(xT)[:, unstriped(offs)], 0, "e4m3")
    z = sum(f64(gate)[d, :1] * h[:, unstriped(p)] for d, p in enumerate((pos1, pos2, pos3)))
    return mxq(f64(w2), 0, "e4m3").T @ mxq(z, 0, "e4m3")

@@ -1,0 +1,223 @@
+from contextlib import ExitStack
+
+import concourse.mybir as mybir
+from concourse.masks import make_identity
+
+F32 = mybir.dt.float32
+BF16 = mybir.dt.bfloat16
+U32 = mybir.dt.uint32
+U16 = mybir.dt.uint16
+U8 = mybir.dt.uint8
+FP8X4 = mybir.dt.float8_e4m3fn_x4
+COPY = mybir.ActivationFunctionType.Copy
+MULT = mybir.AluOpType.mult
+
+P = 128
+K, T, D, S, V, H, N = 1024, 1024, 3, 512, 256, 1024, 128
+PASSES = K // 512
+GROUPS = H // 512
+CUTS = (0, 128, 256)
+
+FLOPS = 2 * K * H * S + 2 * H * N * V
+
+
+def tile_picked_sage_none_e_kernel(tc, xT, w1, w2, gate, offs, pos1, pos2, pos3, out):
+    nc = tc.nc
+    with ExitStack() as ctx:
+        lists = ctx.enter_context(tc.tile_pool(name="lists", bufs=1))
+        keep = ctx.enter_context(tc.tile_pool(name="keep", bufs=1))
+        hpool = ctx.enter_context(tc.tile_pool(name="hpool", bufs=4))
+        ps_h = ctx.enter_context(tc.psum_pool(name="ps_h", bufs=4))
+        ps_z = ctx.enter_context(tc.psum_pool(name="ps_z", bufs=2))
+        ps_w = ctx.enter_context(tc.psum_pool(name="ps_w", bufs=1))
+        ps_o = ctx.enter_context(tc.psum_pool(name="ps_o", bufs=1))
+
+        offs_t = lists.tile([P, S // 16], U16, name="offs_t")
+        pos_t = [lists.tile([P, V // 16], U16, name=f"pos_t{d}") for d in range(D)]
+
+        ident = keep.tile([P, P], F32, name="ident")
+        make_identity(nc, ident[:])
+
+        x_view = xT.rearrange("(s p u e) t -> s u p e t", s=PASSES, p=P, u=2, e=2)
+        x_raw = {}
+        order = [(s, u) for s in range(PASSES) for u in range(2)]
+        for n, (s, u) in enumerate(order):
+            parts = 2 if n in (0, 3) else 1
+            w = T // parts
+            for q in range(parts):
+                t = keep.tile([P, 2, w], F32, name=f"x_raw{s}{u}{q}")
+                nc.sync.dma_start(t[:], x_view[s, u][:, :, q * w : (q + 1) * w])
+                x_raw[s, u, q] = t
+                if n == 0 and q == 0:
+                    nc.sync.dma_start(offs_t[:], offs)
+        w1_view = w1.rearrange("(s p j) c -> s p j c", s=PASSES, p=P, j=4)
+        CW = 256
+        w1_raw = {}
+        gate_t = keep.tile([P, D, V], F32, name="gate_t")
+        for c in range(H // CW):
+            for s in range(PASSES):
+                t = keep.tile([P, 4, CW], F32, name=f"w1_raw{c}{s}")
+                nc.sync.dma_start(t[:], w1_view[s][:, :, c * CW : (c + 1) * CW])
+                w1_raw[c, s] = t
+            if c == 0:
+                for d, src in enumerate((pos1, pos2, pos3)):
+                    nc.sync.dma_start(pos_t[d][:], src)
+                    nc.sync.dma_start(gate_t[:, d, :], gate[d])
+            if c == 1:
+                w2_raw = keep.tile([P, GROUPS, 4, N], F32, name="w2_raw")
+                nc.sync.dma_start(w2_raw[:], w2.rearrange("(g p j) n -> p g j n", g=GROUPS, j=4))
+
+        x_codes, x_scales = [], []
+        for s in range(PASSES):
+            xg = keep.tile([P, S, 4], BF16, name=f"xg{s}", align_bytes=64)
+            xg_words = xg[:].rearrange("p n k -> p (n k)").bitcast(U32).rearrange("p (n u) -> p n u", u=2)
+            for u in range(2):
+                xb = keep.tile([P, T, 2], BF16, name=f"xb{s}{u}")
+                q = 0
+                while (s, u, q) in x_raw:
+                    raw = x_raw[s, u, q]
+                    w = raw.shape[2]
+                    half = w // 2
+                    nc.vector.tensor_copy(xb[:, q * w : q * w + half, :], raw[:, :, 0:half].rearrange("p e t -> p t e"))
+                    nc.scalar.activation(
+                        xb[:, q * w + half : (q + 1) * w, :], raw[:, :, half:w].rearrange("p e t -> p t e"), COPY
+                    )
+                    q += 1
+                window = xb[:].rearrange("p t e -> p (t e)").bitcast(U32)
+                nc.vector.tensor_copy(xg_words[:, :, u], window.indirect(offs_t[:]))
+            codes = keep.tile([P, S], U32, name=f"x_codes{s}", align_bytes=64)
+            scales = keep.tile([P, S], U8, name=f"x_scales{s}", align_bytes=64)
+            nc.vector.quantize_mx(
+                out=codes[:].bitcast(FP8X4), scales=scales[:], in_=xg[:].rearrange("p n k -> p (n k)")
+            )
+            x_codes.append(codes)
+            x_scales.append(scales)
+
+        def cast4(engine, dst, src):
+            o = dst.rearrange("p (q i) j -> p q j i", i=4)
+            i = src.rearrange("p j (q i) -> p q j i", i=4)
+            if engine == "v":
+                nc.vector.tensor_copy(o, i)
+            else:
+                nc.scalar.activation(o, i, COPY)
+
+        zT = keep.tile([P, 2, H], BF16, name="zT")
+        acc_o = ps_o.tile([N, V], F32, name="acc_o")
+        w2_c = keep.tile([P, GROUPS, N], U32, name="w2_c", align_bytes=64)
+        w2_s = keep.tile([P, GROUPS, N], U8, name="w2_s", align_bytes=64)
+        NC = H // CW
+        h_tiles = {}
+        z_codes = {}
+
+        def produce(c):
+            codes_c, scales_c = [], []
+            for s in range(PASSES):
+                grouped = keep.tile([P, CW, 4], BF16, name=f"w1_g{c}{s}", align_bytes=64)
+                codes = keep.tile([P, CW], U32, name=f"w1_codes{c}{s}", align_bytes=64)
+                scales = keep.tile([P, CW], U8, name=f"w1_scales{c}{s}", align_bytes=64)
+                if c == 0:
+                    cuts, who, quants = (0, 128, 256), ("ss", "vs")[s], (0, 128, 256)
+                else:
+                    cuts, who, quants = CUTS, "vs", (0, 256)
+                for n, e in enumerate(who):
+                    cols = slice(cuts[n], cuts[n + 1])
+                    if cuts[n + 1] > cuts[n]:
+                        cast4(e, grouped[:, cols, :], w1_raw[c, s][:, :, cols])
+                for n in range(len(quants) - 1):
+                    cols = slice(quants[n], quants[n + 1])
+                    nc.vector.quantize_mx(
+                        out=codes[:, cols].bitcast(FP8X4),
+                        scales=scales[:, cols],
+                        in_=grouped[:, cols, :].rearrange("p n k -> p (n k)"),
+                    )
+                codes_c.append(codes)
+                scales_c.append(scales)
+            for hf in range(CW // P):
+                r = c * (CW // P) + hf
+                cols = slice(128 * hf, 128 * hf + 128)
+                acc = ps_h.tile([P, S], F32, name="acc")
+                for s in range(PASSES):
+                    nc.tensor.matmul_mx(
+                        out=acc[:],
+                        lhsT=codes_c[s][:, cols].bitcast(FP8X4),
+                        lhsT_scale=scales_c[s][:, cols],
+                        rhs=x_codes[s][:].bitcast(FP8X4),
+                        rhs_scale=x_scales[s][:],
+                        start=(s == 0),
+                        stop=(s == PASSES - 1),
+                    )
+                h = hpool.tile([P, S], F32, name="h")
+                nc.scalar.activation(h[:], acc[:], COPY)
+                h_tiles[r] = h
+
+        def aggregate(c):
+            zps = ps_z.tile([P, 2, 2, P], F32, name="zps")
+            for hf in range(2):
+                r = 2 * c + hf
+                picked = []
+                for d in range(D):
+                    g = hpool.tile([P, V], F32, name=f"picked{d}")
+                    nc.vector.tensor_tensor(g[:], h_tiles[r][:].indirect(pos_t[d][:]), gate_t[:, d, :], MULT)
+                    picked.append(g)
+                for vh in range(2):
+                    for d in range(D):
+                        nc.tensor.matmul(
+                            zps[:, vh, hf, :],
+                            picked[d][:, vh * P : vh * P + P],
+                            ident[:],
+                            start=(d == 0),
+                            stop=(d == D - 1),
+                            is_transpose=True,
+                        )
+            nc.scalar.activation(zT[:, :, c * CW : (c + 1) * CW], zps[:].rearrange("p h r i -> p h (r i)"), COPY)
+
+        def second_operand(g):
+            zw = ps_w.tile([P, 2, 2, P], F32, name="zw")
+            for vh in range(2):
+                words = zT[:, vh, g * 512 : (g + 1) * 512].bitcast(F32)
+                for u in range(2):
+                    nc.tensor.transpose(zw[:, vh, u, :], words[:, u::2], ident[:])
+            zq = keep.tile([P, 2, P, 4], BF16, name=f"zq{g}", align_bytes=64)
+            zq_words = zq[:].rearrange("p h v k -> p (h v k)").bitcast(F32)
+            nc.scalar.copy(
+                zq_words.rearrange("p (h v u) -> p h v u", h=2, u=2), zw[:].rearrange("p h u v -> p h v u")
+            )
+            zc = keep.tile([P, V], U32, name=f"zc{g}", align_bytes=64)
+            zs = keep.tile([P, V], U8, name=f"zs{g}", align_bytes=64)
+            nc.vector.quantize_mx(
+                out=zc[:].bitcast(FP8X4), scales=zs[:], in_=zq[:].rearrange("p h v k -> p (h v k)")
+            )
+            z_codes[g] = (zc, zs)
+
+        def weights2():
+            w2_g = keep.tile([P, GROUPS, N, 4], BF16, name="w2_g", align_bytes=64)
+            for g in range(GROUPS):
+                cast4("s", w2_g[:, g], w2_raw[:, g])
+            nc.vector.quantize_mx(
+                out=w2_c[:].rearrange("p g n -> p (g n)").bitcast(FP8X4),
+                scales=w2_s[:].rearrange("p g n -> p (g n)"),
+                in_=w2_g[:].rearrange("p g n k -> p (g n k)"),
+            )
+
+        produce(0)
+        for c in range(NC):
+            if c + 1 < NC:
+                produce(c + 1)
+            aggregate(c)
+            if c == 2:
+                second_operand(0)
+                weights2()
+        second_operand(1)
+        for g, (zc, zs) in enumerate((z_codes[0], z_codes[1])):
+            nc.tensor.matmul_mx(
+                out=acc_o[:],
+                lhsT=w2_c[:, g, :].bitcast(FP8X4),
+                lhsT_scale=w2_s[:, g, :],
+                rhs=zc[:].bitcast(FP8X4),
+                rhs_scale=zs[:],
+                start=(g == 0),
+                stop=(g == GROUPS - 1),
+            )
+        res = keep.tile([N, V], F32, name="res")
+        nc.scalar.activation(res[:], acc_o[:], COPY)
+        nc.sync.dma_start(out, res[:])

@@ -16,7 +16,8 @@ P = 128
 K, T, D, S, V, H, N = 1024, 1024, 3, 512, 256, 1024, 128
 PASSES = K // 512
 GROUPS = H // 512
-CUTS = (0, 128, 256)
+CHUNKS = ((0, 128), (128, 128), (256, 256), (512, 256), (768, 256))
+W1_CAST = ["ss","ss","sv","vs","vs"]
 
 FLOPS = 2 * K * H * S + 2 * H * N * V
 
@@ -26,72 +27,55 @@ def tile_picked_sage_none_e_kernel(tc, xT, w1, w2, gate, offs, pos1, pos2, pos3,
     with ExitStack() as ctx:
         lists = ctx.enter_context(tc.tile_pool(name="lists", bufs=1))
         keep = ctx.enter_context(tc.tile_pool(name="keep", bufs=1))
-        hpool = ctx.enter_context(tc.tile_pool(name="hpool", bufs=4))
-        ps_h = ctx.enter_context(tc.psum_pool(name="ps_h", bufs=4))
+        picks = ctx.enter_context(tc.tile_pool(name="picks", bufs=4))
+        ps_h = ctx.enter_context(tc.psum_pool(name="ps_h", bufs=3))
         ps_z = ctx.enter_context(tc.psum_pool(name="ps_z", bufs=2))
-        ps_w = ctx.enter_context(tc.psum_pool(name="ps_w", bufs=1))
-        ps_o = ctx.enter_context(tc.psum_pool(name="ps_o", bufs=1))
+        ps_1 = ctx.enter_context(tc.psum_pool(name="ps_1", bufs=1))
 
         offs_t = lists.tile([P, S // 16], U16, name="offs_t")
         pos_t = [lists.tile([P, V // 16], U16, name=f"pos_t{d}") for d in range(D)]
-
         ident = keep.tile([P, P], F32, name="ident")
         make_identity(nc, ident[:])
 
         x_view = xT.rearrange("(s p u e) t -> s u p e t", s=PASSES, p=P, u=2, e=2)
-        x_raw = {}
-        order = [(s, u) for s in range(PASSES) for u in range(2)]
-        for n, (s, u) in enumerate(order):
-            parts = 2 if n in (0, 3) else 1
-            w = T // parts
-            for q in range(parts):
-                t = keep.tile([P, 2, w], F32, name=f"x_raw{s}{u}{q}")
-                nc.sync.dma_start(t[:], x_view[s, u][:, :, q * w : (q + 1) * w])
-                x_raw[s, u, q] = t
-                if n == 0 and q == 0:
-                    nc.sync.dma_start(offs_t[:], offs)
         w1_view = w1.rearrange("(s p j) c -> s p j c", s=PASSES, p=P, j=4)
-        CW = 256
-        w1_raw = {}
+        x_raw, w1_raw = {}, {}
         gate_t = keep.tile([P, D, V], F32, name="gate_t")
-        for c in range(H // CW):
-            for s in range(PASSES):
-                t = keep.tile([P, 4, CW], F32, name=f"w1_raw{c}{s}")
-                nc.sync.dma_start(t[:], w1_view[s][:, :, c * CW : (c + 1) * CW])
-                w1_raw[c, s] = t
-            if c == 0:
-                for d, src in enumerate((pos1, pos2, pos3)):
-                    nc.sync.dma_start(pos_t[d][:], src)
-                    nc.sync.dma_start(gate_t[:, d, :], gate[d])
-            if c == 1:
-                w2_raw = keep.tile([P, GROUPS, 4, N], F32, name="w2_raw")
-                nc.sync.dma_start(w2_raw[:], w2.rearrange("(g p j) n -> p g j n", g=GROUPS, j=4))
 
-        x_codes, x_scales = [], []
-        for s in range(PASSES):
-            xg = keep.tile([P, S, 4], BF16, name=f"xg{s}", align_bytes=64)
-            xg_words = xg[:].rearrange("p n k -> p (n k)").bitcast(U32).rearrange("p (n u) -> p n u", u=2)
-            for u in range(2):
-                xb = keep.tile([P, T, 2], BF16, name=f"xb{s}{u}")
-                q = 0
-                while (s, u, q) in x_raw:
-                    raw = x_raw[s, u, q]
-                    w = raw.shape[2]
-                    half = w // 2
-                    nc.vector.tensor_copy(xb[:, q * w : q * w + half, :], raw[:, :, 0:half].rearrange("p e t -> p t e"))
-                    nc.scalar.activation(
-                        xb[:, q * w + half : (q + 1) * w, :], raw[:, :, half:w].rearrange("p e t -> p t e"), COPY
-                    )
-                    q += 1
-                window = xb[:].rearrange("p t e -> p (t e)").bitcast(U32)
-                nc.vector.tensor_copy(xg_words[:, :, u], window.indirect(offs_t[:]))
-            codes = keep.tile([P, S], U32, name=f"x_codes{s}", align_bytes=64)
-            scales = keep.tile([P, S], U8, name=f"x_scales{s}", align_bytes=64)
-            nc.vector.quantize_mx(
-                out=codes[:].bitcast(FP8X4), scales=scales[:], in_=xg[:].rearrange("p n k -> p (n k)")
-            )
-            x_codes.append(codes)
-            x_scales.append(scales)
+        def load_x(s, u, parts):
+            w = T // parts
+            for n in range(parts):
+                t = keep.tile([P, 2, w], F32, name=f"x_raw{s}{u}{n}")
+                nc.sync.dma_start(t[:], x_view[s, u][:, :, n * w : (n + 1) * w])
+                x_raw[s, u, n] = t
+
+        def load_w1(c, s):
+            c0, width = CHUNKS[c]
+            t = keep.tile([P, 4, width], F32, name=f"w1_raw{c}{s}")
+            nc.sync.dma_start(t[:], w1_view[s][:, :, c0 : c0 + width])
+            w1_raw[c, s] = t
+
+        nc.sync.dma_start(offs_t[:], offs)
+        load_x(0, 0, 2)
+        load_w1(0, 0)
+        load_x(0, 1, 1)
+        load_w1(0, 1)
+        load_x(1, 0, 1)
+        load_x(1, 1, 2)
+        load_w1(1, 0)
+        load_w1(1, 1)
+        for d, src in enumerate((pos1, pos2, pos3)):
+            nc.sync.dma_start(pos_t[d][:], src)
+        nc.sync.dma_start(gate_t[:, 0, :], gate[0])
+        load_w1(2, 0)
+        load_w1(2, 1)
+        for d in range(1, D):
+            nc.sync.dma_start(gate_t[:, d, :], gate[d])
+        for c in (3, 4):
+            for s in range(PASSES):
+                load_w1(c, s)
+        w2_raw = keep.tile([P, GROUPS, 4, N], F32, name="w2_raw")
+        nc.sync.dma_start(w2_raw[:], w2.rearrange("(g p j) n -> p g j n", g=GROUPS, j=4))
 
         def cast4(engine, dst, src):
             o = dst.rearrange("p (q i) j -> p q j i", i=4)
@@ -101,93 +85,119 @@ def tile_picked_sage_none_e_kernel(tc, xT, w1, w2, gate, offs, pos1, pos2, pos3,
             else:
                 nc.scalar.activation(o, i, COPY)
 
-        zT = keep.tile([P, 2, H], BF16, name="zT")
-        acc_o = ps_o.tile([N, V], F32, name="acc_o")
-        w2_c = keep.tile([P, GROUPS, N], U32, name="w2_c", align_bytes=64)
-        w2_s = keep.tile([P, GROUPS, N], U8, name="w2_s", align_bytes=64)
-        NC = H // CW
-        h_tiles = {}
-        z_codes = {}
+        x_codes, x_scales, xg = {}, {}, {}
 
-        def produce(c):
-            codes_c, scales_c = [], []
+        def pick_pairs(s, u):
+            if u == 0:
+                xg[s] = keep.tile([P, S, 4], BF16, name=f"xg{s}", align_bytes=64)
+            xg_words = xg[s][:].rearrange("p n k -> p (n k)").bitcast(U32).rearrange("p (n u) -> p n u", u=2)
+            xb = keep.tile([P, T, 2], BF16, name=f"xb{s}{u}")
+            parts = 2 if (s, u, 1) in x_raw else 1
+            w = T // parts
+            for n in range(parts):
+                raw = x_raw[s, u, n]
+                mid = 0 if (s, u, n) == (1, 1, 1) else w * 3 // 4
+                for engine, a, b in (("s", mid, w), ("v", 0, mid)):
+                    if a == b:
+                        continue
+                    dst, src = xb[:, n * w + a : n * w + b, :], raw[:, :, a:b].rearrange("p e t -> p t e")
+                    if engine == "v":
+                        nc.vector.tensor_copy(dst, src)
+                    else:
+                        nc.scalar.activation(dst, src, COPY)
+            window = xb[:].rearrange("p t e -> p (t e)").bitcast(U32)
+            nc.vector.tensor_copy(xg_words[:, :, u], window.indirect(offs_t[:]))
+            if u == 1:
+                codes = keep.tile([P, S], U32, name=f"x_codes{s}", align_bytes=64)
+                scales = keep.tile([P, S], U8, name=f"x_scales{s}", align_bytes=64)
+                nc.vector.quantize_mx(
+                    out=codes[:].bitcast(FP8X4), scales=scales[:], in_=xg[s][:].rearrange("p n k -> p (n k)")
+                )
+                x_codes[s], x_scales[s] = codes, scales
+
+        w1_codes, w1_scales, h_tiles, z_codes = {}, {}, {}, {}
+
+        def quantise_w1(c):
+            start, width = CHUNKS[c]
+            grouped = keep.tile([P, PASSES, width, 4], BF16, name=f"w1_g{c}", align_bytes=64)
+            codes = keep.tile([P, PASSES, width], U32, name=f"w1_codes{c}", align_bytes=64)
+            scales = keep.tile([P, PASSES, width], U8, name=f"w1_scales{c}", align_bytes=64)
             for s in range(PASSES):
-                grouped = keep.tile([P, CW, 4], BF16, name=f"w1_g{c}{s}", align_bytes=64)
-                codes = keep.tile([P, CW], U32, name=f"w1_codes{c}{s}", align_bytes=64)
-                scales = keep.tile([P, CW], U8, name=f"w1_scales{c}{s}", align_bytes=64)
-                if c == 0:
-                    cuts, who, quants = (0, 128, 256), ("ss", "vs")[s], (0, 128, 256)
-                else:
-                    cuts, who, quants = CUTS, "vs", (0, 256)
-                for n, e in enumerate(who):
-                    cols = slice(cuts[n], cuts[n + 1])
-                    if cuts[n + 1] > cuts[n]:
-                        cast4(e, grouped[:, cols, :], w1_raw[c, s][:, :, cols])
-                for n in range(len(quants) - 1):
-                    cols = slice(quants[n], quants[n + 1])
-                    nc.vector.quantize_mx(
-                        out=codes[:, cols].bitcast(FP8X4),
-                        scales=scales[:, cols],
-                        in_=grouped[:, cols, :].rearrange("p n k -> p (n k)"),
-                    )
-                codes_c.append(codes)
-                scales_c.append(scales)
-            for hf in range(CW // P):
-                r = c * (CW // P) + hf
-                cols = slice(128 * hf, 128 * hf + 128)
+                cast4(W1_CAST[c][s], grouped[:, s], w1_raw[c, s][:])
+            nc.vector.quantize_mx(
+                out=codes[:].rearrange("p s n -> p (s n)").bitcast(FP8X4),
+                scales=scales[:].rearrange("p s n -> p (s n)"),
+                in_=grouped[:].rearrange("p s n k -> p (s n k)"),
+            )
+            w1_codes[c], w1_scales[c] = codes, scales
+
+        def project(c):
+            start, width = CHUNKS[c]
+            for first in range(0, width, P):
+                r = (start + first) // P
+                cols = slice(first, first + P)
                 acc = ps_h.tile([P, S], F32, name="acc")
                 for s in range(PASSES):
                     nc.tensor.matmul_mx(
                         out=acc[:],
-                        lhsT=codes_c[s][:, cols].bitcast(FP8X4),
-                        lhsT_scale=scales_c[s][:, cols],
+                        lhsT=w1_codes[c][:, s, cols].bitcast(FP8X4),
+                        lhsT_scale=w1_scales[c][:, s, cols],
                         rhs=x_codes[s][:].bitcast(FP8X4),
                         rhs_scale=x_scales[s][:],
                         start=(s == 0),
                         stop=(s == PASSES - 1),
                     )
-                h = hpool.tile([P, S], F32, name="h")
+                h = keep.tile([P, S], F32, name=f"h{r}")
                 nc.scalar.activation(h[:], acc[:], COPY)
                 h_tiles[r] = h
 
-        def aggregate(c):
-            zps = ps_z.tile([P, 2, 2, P], F32, name="zps")
-            for hf in range(2):
-                r = 2 * c + hf
-                picked = []
-                for d in range(D):
-                    g = hpool.tile([P, V], F32, name=f"picked{d}")
-                    nc.vector.tensor_tensor(g[:], h_tiles[r][:].indirect(pos_t[d][:]), gate_t[:, d, :], MULT)
-                    picked.append(g)
+        def produce(c):
+            if c > 0:
+                quantise_w1(c)
+            project(c)
+
+        zT = keep.tile([P, 2, H], BF16, name="zT")
+        w2_c = keep.tile([P, GROUPS, N], U32, name="w2_c", align_bytes=64)
+        w2_s = keep.tile([P, GROUPS, N], U8, name="w2_s", align_bytes=64)
+
+        def pick_h(r, d):
+            g = picks.tile([P, V], F32, name=f"picked{d}")
+            nc.vector.tensor_tensor(g[:], h_tiles[r][:].indirect(pos_t[d][:]), gate_t[:, d, :], MULT)
+            return g
+
+        def add_turned(dst, g, vh, d):
+            nc.tensor.matmul(
+                dst, g[:, vh * P : vh * P + P], ident[:], start=(d == 0), stop=(d == D - 1), is_transpose=True
+            )
+
+        def aggregate(rows):
+            zps = ps_z.tile([P, 2, len(rows), P], F32, name="zps")
+            for n, r in enumerate(rows):
+                picked = [pick_h(r, d) for d in range(D)]
                 for vh in range(2):
                     for d in range(D):
-                        nc.tensor.matmul(
-                            zps[:, vh, hf, :],
-                            picked[d][:, vh * P : vh * P + P],
-                            ident[:],
-                            start=(d == 0),
-                            stop=(d == D - 1),
-                            is_transpose=True,
-                        )
-            nc.scalar.activation(zT[:, :, c * CW : (c + 1) * CW], zps[:].rearrange("p h r i -> p h (r i)"), COPY)
+                        add_turned(zps[:, vh, n, :], picked[d], vh, d)
+            first, last = rows[0] * P, rows[-1] * P + P
+            nc.scalar.activation(zT[:, :, first:last], zps[:].rearrange("p h r i -> p h (r i)"), COPY)
 
         def second_operand(g):
-            zw = ps_w.tile([P, 2, 2, P], F32, name="zw")
+            zw = ps_1.tile([P, 2, 2, P], F32, name="zw")
             for vh in range(2):
                 words = zT[:, vh, g * 512 : (g + 1) * 512].bitcast(F32)
                 for u in range(2):
                     nc.tensor.transpose(zw[:, vh, u, :], words[:, u::2], ident[:])
-            zq = keep.tile([P, 2, P, 4], BF16, name=f"zq{g}", align_bytes=64)
+            zq = keep.tile([P, 2, P, 4], BF16, name="zq", align_bytes=64)
             zq_words = zq[:].rearrange("p h v k -> p (h v k)").bitcast(F32)
             nc.scalar.copy(
                 zq_words.rearrange("p (h v u) -> p h v u", h=2, u=2), zw[:].rearrange("p h u v -> p h v u")
             )
-            zc = keep.tile([P, V], U32, name=f"zc{g}", align_bytes=64)
-            zs = keep.tile([P, V], U8, name=f"zs{g}", align_bytes=64)
+            zc = keep.tile([P, V], U32, name="zc", align_bytes=64)
+            zs = keep.tile([P, V], U8, name="zs", align_bytes=64)
             nc.vector.quantize_mx(
                 out=zc[:].bitcast(FP8X4), scales=zs[:], in_=zq[:].rearrange("p h v k -> p (h v k)")
             )
-            z_codes[g] = (zc, zs)
+            for vh in range(2):
+                z_codes[g, vh] = (zc[:, vh * P : vh * P + P], zs[:, vh * P : vh * P + P])
 
         def weights2():
             w2_g = keep.tile([P, GROUPS, N, 4], BF16, name="w2_g", align_bytes=64)
@@ -199,25 +209,81 @@ def tile_picked_sage_none_e_kernel(tc, xT, w1, w2, gate, offs, pos1, pos2, pos3,
                 in_=w2_g[:].rearrange("p g n k -> p (g n k)"),
             )
 
-        produce(0)
-        for c in range(NC):
-            if c + 1 < NC:
-                produce(c + 1)
-            aggregate(c)
-            if c == 2:
-                second_operand(0)
-                weights2()
-        second_operand(1)
-        for g, (zc, zs) in enumerate((z_codes[0], z_codes[1])):
-            nc.tensor.matmul_mx(
-                out=acc_o[:],
-                lhsT=w2_c[:, g, :].bitcast(FP8X4),
-                lhsT_scale=w2_s[:, g, :],
-                rhs=zc[:].bitcast(FP8X4),
-                rhs_scale=zs[:],
-                start=(g == 0),
-                stop=(g == GROUPS - 1),
-            )
-        res = keep.tile([N, V], F32, name="res")
-        nc.scalar.activation(res[:], acc_o[:], COPY)
-        nc.sync.dma_start(out, res[:])
+        def tail():
+            r = H // P - 1
+            banks = [ps_h.tile([P, S], F32, name="acc") for vh in range(2)]
+            for vh in range(2):
+                for d in range(D):
+                    g = picks.tile([P, P], F32, name=f"half{d}")
+                    part = pos_t[d][:, vh * (P // 16) : (vh + 1) * (P // 16)]
+                    nc.vector.tensor_tensor(
+                        g[:], h_tiles[r][:].indirect(part), gate_t[:, d, vh * P : vh * P + P], MULT
+                    )
+                    nc.tensor.matmul(
+                        banks[vh][:, 0:P], g[:], ident[:], start=(d == 0), stop=(d == D - 1), is_transpose=True
+                    )
+            for vh in range(2):
+                dst, src = zT[:, vh, r * P : r * P + P], banks[vh][:, 0:P]
+                if vh == 0:
+                    nc.scalar.activation(dst, src, COPY)
+                else:
+                    nc.vector.tensor_copy(dst, src)
+            res = keep.tile([N, V], F32, name="res")
+            for vh in range(2):
+                zw = ps_h.tile([P, S], F32, name="acc")
+                words = zT[:, vh, 512:1024].bitcast(F32)
+                for u in range(2):
+                    nc.tensor.transpose(zw[:, u * P : u * P + P], words[:, u::2], ident[:])
+                zq = keep.tile([P, P, 4], BF16, name=f"zq_tail{vh}", align_bytes=64)
+                dst = zq[:].rearrange("p v k -> p (v k)").bitcast(F32).rearrange("p (v u) -> p v u", u=2)
+                src = zw[:, 0 : 2 * P].rearrange("p (u v) -> p v u", u=2)
+                if vh == 0:
+                    nc.scalar.copy(dst, src)
+                else:
+                    nc.vector.tensor_copy(dst, src)
+                zc = keep.tile([P, P], U32, name=f"zc_tail{vh}", align_bytes=64)
+                zs = keep.tile([P, P], U8, name=f"zs_tail{vh}", align_bytes=64)
+                nc.vector.quantize_mx(
+                    out=zc[:].bitcast(FP8X4), scales=zs[:], in_=zq[:].rearrange("p v k -> p (v k)")
+                )
+                z_codes[1, vh] = (zc[:], zs[:])
+                acc_o = ps_1.tile([N, P], F32, name=f"acc_o{vh}")
+                for g in range(GROUPS):
+                    zc, zs = z_codes[g, vh]
+                    nc.tensor.matmul_mx(
+                        out=acc_o[:],
+                        lhsT=w2_c[:, g, :].bitcast(FP8X4),
+                        lhsT_scale=w2_s[:, g, :],
+                        rhs=zc.bitcast(FP8X4),
+                        rhs_scale=zs,
+                        start=(g == 0),
+                        stop=(g == GROUPS - 1),
+                    )
+                cols = slice(vh * P, vh * P + P)
+                if vh == 0:
+                    nc.scalar.activation(res[:, cols], acc_o[:], COPY)
+                else:
+                    nc.vector.tensor_copy(res[:, cols], acc_o[:])
+                nc.sync.dma_start(out[:, cols], res[:, cols])
+
+        pick_pairs(0, 0)
+        quantise_w1(0)
+        pick_pairs(0, 1)
+        pick_pairs(1, 0)
+        pick_pairs(1, 1)
+        project(0)
+        quantise_w1(1)
+        quantise_w1(2)
+        project(1)
+        project(2)
+        quantise_w1(3)
+        aggregate((0, 1))
+        project(3)
+        weights2()
+        quantise_w1(4)
+        aggregate((2, 3))
+        project(4)
+        aggregate((4, 5))
+        aggregate((6,))
+        second_operand(0)
+        tail()

@@ -55,23 +55,19 @@ def tile_picked_sage_none_e_kernel(tc, xT, w1, w2, gate, offs, pos1, pos2, pos3,
             nc.sync.dma_start(t[:], w1_view[s][:, :, c0 : c0 + width])
             w1_raw[c, s] = t
 
-        nc.sync.dma_start(offs_t[:], offs)
         load_x(0, 0, 2)
+        nc.sync.dma_start(offs_t[:], offs)
         load_w1(0, 0)
         load_x(0, 1, 1)
         load_w1(0, 1)
         load_x(1, 0, 1)
         load_x(1, 1, 2)
-        load_w1(1, 0)
-        load_w1(1, 1)
         for d, src in enumerate((pos1, pos2, pos3)):
             nc.sync.dma_start(pos_t[d][:], src)
-        nc.sync.dma_start(gate_t[:, 0, :], gate[0])
-        load_w1(2, 0)
-        load_w1(2, 1)
-        for d in range(1, D):
-            nc.sync.dma_start(gate_t[:, d, :], gate[d])
-        for c in (3, 4):
+        load_w1(1, 0)
+        load_w1(1, 1)
+        nc.sync.dma_start(gate_t[:], gate.rearrange("d p v -> p d v"))
+        for c in (2, 3, 4):
             for s in range(PASSES):
                 load_w1(c, s)
         w2_raw = keep.tile([P, GROUPS, 4, N], F32, name="w2_raw")
@@ -151,10 +147,23 @@ def tile_picked_sage_none_e_kernel(tc, xT, w1, w2, gate, offs, pos1, pos2, pos3,
                 nc.scalar.activation(h[:], acc[:], COPY)
                 h_tiles[r] = h
 
-        def produce(c):
-            if c > 0:
-                quantise_w1(c)
-            project(c)
+        def project_first():
+            h = keep.tile([P, S], F32, name="h0")
+            for a in range(2):
+                part = slice(a * 256, a * 256 + 256)
+                acc = ps_h.tile([P, S], F32, name="acc")
+                for s in range(PASSES):
+                    nc.tensor.matmul_mx(
+                        out=acc[:, 0:256],
+                        lhsT=w1_codes[0][:, s, :].bitcast(FP8X4),
+                        lhsT_scale=w1_scales[0][:, s, :],
+                        rhs=x_codes[s][:, part].bitcast(FP8X4),
+                        rhs_scale=x_scales[s][:, part],
+                        start=(s == 0),
+                        stop=(s == PASSES - 1),
+                    )
+                nc.scalar.activation(h[:, part], acc[:, 0:256], COPY)
+            h_tiles[0] = h
 
         zT = keep.tile([P, 2, H], BF16, name="zT")
         w2_c = keep.tile([P, GROUPS, N], U32, name="w2_c", align_bytes=64)
@@ -271,7 +280,7 @@ def tile_picked_sage_none_e_kernel(tc, xT, w1, w2, gate, offs, pos1, pos2, pos3,
         pick_pairs(0, 1)
         pick_pairs(1, 0)
         pick_pairs(1, 1)
-        project(0)
+        project_first()
         quantise_w1(1)
         quantise_w1(2)
         project(1)

from contextlib import ExitStack

import concourse.mybir as mybir
from concourse.masks import make_identity

F32 = mybir.dt.float32
BF16 = mybir.dt.bfloat16
U32 = mybir.dt.uint32
U16 = mybir.dt.uint16
U8 = mybir.dt.uint8
FP8X4 = mybir.dt.float8_e4m3fn_x4
COPY = mybir.ActivationFunctionType.Copy
MULT = mybir.AluOpType.mult

P = 128
K, T, D, S, V, H, N = 1024, 1024, 3, 512, 256, 1024, 128
PASSES = K // 512
GROUPS = H // 512
CHUNKS = ((0, 128), (128, 128), (256, 256), (512, 256), (768, 256))
W1_CAST = ["ss","ss","sv","vs","vs"]

FLOPS = 2 * K * H * S + 2 * H * N * V


def tile_picked_sage_none_e_kernel(tc, xT, w1, w2, gate, offs, pos1, pos2, pos3, out):
    nc = tc.nc
    with ExitStack() as ctx:
        lists = ctx.enter_context(tc.tile_pool(name="lists", bufs=1))
        keep = ctx.enter_context(tc.tile_pool(name="keep", bufs=1))
        picks = ctx.enter_context(tc.tile_pool(name="picks", bufs=4))
        ps_h = ctx.enter_context(tc.psum_pool(name="ps_h", bufs=3))
        ps_z = ctx.enter_context(tc.psum_pool(name="ps_z", bufs=2))
        ps_1 = ctx.enter_context(tc.psum_pool(name="ps_1", bufs=1))

        offs_t = lists.tile([P, S // 16], U16, name="offs_t")
        pos_t = [lists.tile([P, V // 16], U16, name=f"pos_t{d}") for d in range(D)]
        ident = keep.tile([P, P], F32, name="ident")
        make_identity(nc, ident[:])

        x_view = xT.rearrange("(s p u e) t -> s u p e t", s=PASSES, p=P, u=2, e=2)
        w1_view = w1.rearrange("(s p j) c -> s p j c", s=PASSES, p=P, j=4)
        x_raw, w1_raw = {}, {}
        gate_t = keep.tile([P, D, V], F32, name="gate_t")

        def load_x(s, u, parts):
            w = T // parts
            for n in range(parts):
                t = keep.tile([P, 2, w], F32, name=f"x_raw{s}{u}{n}")
                nc.sync.dma_start(t[:], x_view[s, u][:, :, n * w : (n + 1) * w])
                x_raw[s, u, n] = t

        def load_w1(c, s):
            c0, width = CHUNKS[c]
            t = keep.tile([P, 4, width], F32, name=f"w1_raw{c}{s}")
            nc.sync.dma_start(t[:], w1_view[s][:, :, c0 : c0 + width])
            w1_raw[c, s] = t

        load_x(0, 0, 2)
        nc.sync.dma_start(offs_t[:], offs)
        load_w1(0, 0)
        load_x(0, 1, 1)
        load_w1(0, 1)
        load_x(1, 0, 1)
        load_x(1, 1, 2)
        for d, src in enumerate((pos1, pos2, pos3)):
            nc.sync.dma_start(pos_t[d][:], src)
        load_w1(1, 0)
        load_w1(1, 1)
        nc.sync.dma_start(gate_t[:], gate.rearrange("d p v -> p d v"))
        for c in (2, 3, 4):
            for s in range(PASSES):
                load_w1(c, s)
        w2_raw = keep.tile([P, GROUPS, 4, N], F32, name="w2_raw")
        nc.sync.dma_start(w2_raw[:], w2.rearrange("(g p j) n -> p g j n", g=GROUPS, j=4))

        def cast4(engine, dst, src):
            o = dst.rearrange("p (q i) j -> p q j i", i=4)
            i = src.rearrange("p j (q i) -> p q j i", i=4)
            if engine == "v":
                nc.vector.tensor_copy(o, i)
            else:
                nc.scalar.activation(o, i, COPY)

        x_codes, x_scales, xg = {}, {}, {}

        def pick_pairs(s, u):
            if u == 0:
                xg[s] = keep.tile([P, S, 4], BF16, name=f"xg{s}", align_bytes=64)
            xg_words = xg[s][:].rearrange("p n k -> p (n k)").bitcast(U32).rearrange("p (n u) -> p n u", u=2)
            xb = keep.tile([P, T, 2], BF16, name=f"xb{s}{u}")
            parts = 2 if (s, u, 1) in x_raw else 1
            w = T // parts
            for n in range(parts):
                raw = x_raw[s, u, n]
                mid = 0 if (s, u, n) == (1, 1, 1) else w * 3 // 4
                for engine, a, b in (("s", mid, w), ("v", 0, mid)):
                    if a == b:
                        continue
                    dst, src = xb[:, n * w + a : n * w + b, :], raw[:, :, a:b].rearrange("p e t -> p t e")
                    if engine == "v":
                        nc.vector.tensor_copy(dst, src)
                    else:
                        nc.scalar.activation(dst, src, COPY)
            window = xb[:].rearrange("p t e -> p (t e)").bitcast(U32)
            nc.vector.tensor_copy(xg_words[:, :, u], window.indirect(offs_t[:]))
            if u == 1:
                codes = keep.tile([P, S], U32, name=f"x_codes{s}", align_bytes=64)
                scales = keep.tile([P, S], U8, name=f"x_scales{s}", align_bytes=64)
                nc.vector.quantize_mx(
                    out=codes[:].bitcast(FP8X4), scales=scales[:], in_=xg[s][:].rearrange("p n k -> p (n k)")
                )
                x_codes[s], x_scales[s] = codes, scales

        w1_codes, w1_scales, h_tiles, z_codes = {}, {}, {}, {}

        def quantise_w1(c):
            start, width = CHUNKS[c]
            grouped = keep.tile([P, PASSES, width, 4], BF16, name=f"w1_g{c}", align_bytes=64)
            codes = keep.tile([P, PASSES, width], U32, name=f"w1_codes{c}", align_bytes=64)
            scales = keep.tile([P, PASSES, width], U8, name=f"w1_scales{c}", align_bytes=64)
            for s in range(PASSES):
                cast4(W1_CAST[c][s], grouped[:, s], w1_raw[c, s][:])
            nc.vector.quantize_mx(
                out=codes[:].rearrange("p s n -> p (s n)").bitcast(FP8X4),
                scales=scales[:].rearrange("p s n -> p (s n)"),
                in_=grouped[:].rearrange("p s n k -> p (s n k)"),
            )
            w1_codes[c], w1_scales[c] = codes, scales

        def project(c):
            start, width = CHUNKS[c]
            for first in range(0, width, P):
                r = (start + first) // P
                cols = slice(first, first + P)
                acc = ps_h.tile([P, S], F32, name="acc")
                for s in range(PASSES):
                    nc.tensor.matmul_mx(
                        out=acc[:],
                        lhsT=w1_codes[c][:, s, cols].bitcast(FP8X4),
                        lhsT_scale=w1_scales[c][:, s, cols],
                        rhs=x_codes[s][:].bitcast(FP8X4),
                        rhs_scale=x_scales[s][:],
                        start=(s == 0),
                        stop=(s == PASSES - 1),
                    )
                h = keep.tile([P, S], F32, name=f"h{r}")
                nc.scalar.activation(h[:], acc[:], COPY)
                h_tiles[r] = h

        def project_first():
            h = keep.tile([P, S], F32, name="h0")
            for a in range(2):
                part = slice(a * 256, a * 256 + 256)
                acc = ps_h.tile([P, S], F32, name="acc")
                for s in range(PASSES):
                    nc.tensor.matmul_mx(
                        out=acc[:, 0:256],
                        lhsT=w1_codes[0][:, s, :].bitcast(FP8X4),
                        lhsT_scale=w1_scales[0][:, s, :],
                        rhs=x_codes[s][:, part].bitcast(FP8X4),
                        rhs_scale=x_scales[s][:, part],
                        start=(s == 0),
                        stop=(s == PASSES - 1),
                    )
                nc.scalar.activation(h[:, part], acc[:, 0:256], COPY)
            h_tiles[0] = h

        zT = keep.tile([P, 2, H], BF16, name="zT")
        w2_c = keep.tile([P, GROUPS, N], U32, name="w2_c", align_bytes=64)
        w2_s = keep.tile([P, GROUPS, N], U8, name="w2_s", align_bytes=64)

        def pick_h(r, d):
            g = picks.tile([P, V], F32, name=f"picked{d}")
            nc.vector.tensor_tensor(g[:], h_tiles[r][:].indirect(pos_t[d][:]), gate_t[:, d, :], MULT)
            return g

        def add_turned(dst, g, vh, d):
            nc.tensor.matmul(
                dst, g[:, vh * P : vh * P + P], ident[:], start=(d == 0), stop=(d == D - 1), is_transpose=True
            )

        def aggregate(rows):
            zps = ps_z.tile([P, 2, len(rows), P], F32, name="zps")
            for n, r in enumerate(rows):
                picked = [pick_h(r, d) for d in range(D)]
                for vh in range(2):
                    for d in range(D):
                        add_turned(zps[:, vh, n, :], picked[d], vh, d)
            first, last = rows[0] * P, rows[-1] * P + P
            nc.scalar.activation(zT[:, :, first:last], zps[:].rearrange("p h r i -> p h (r i)"), COPY)

        def second_operand(g):
            zw = ps_1.tile([P, 2, 2, P], F32, name="zw")
            for vh in range(2):
                words = zT[:, vh, g * 512 : (g + 1) * 512].bitcast(F32)
                for u in range(2):
                    nc.tensor.transpose(zw[:, vh, u, :], words[:, u::2], ident[:])
            zq = keep.tile([P, 2, P, 4], BF16, name="zq", align_bytes=64)
            zq_words = zq[:].rearrange("p h v k -> p (h v k)").bitcast(F32)
            nc.scalar.copy(
                zq_words.rearrange("p (h v u) -> p h v u", h=2, u=2), zw[:].rearrange("p h u v -> p h v u")
            )
            zc = keep.tile([P, V], U32, name="zc", align_bytes=64)
            zs = keep.tile([P, V], U8, name="zs", align_bytes=64)
            nc.vector.quantize_mx(
                out=zc[:].bitcast(FP8X4), scales=zs[:], in_=zq[:].rearrange("p h v k -> p (h v k)")
            )
            for vh in range(2):
                z_codes[g, vh] = (zc[:, vh * P : vh * P + P], zs[:, vh * P : vh * P + P])

        def weights2():
            w2_g = keep.tile([P, GROUPS, N, 4], BF16, name="w2_g", align_bytes=64)
            for g in range(GROUPS):
                cast4("s", w2_g[:, g], w2_raw[:, g])
            nc.vector.quantize_mx(
                out=w2_c[:].rearrange("p g n -> p (g n)").bitcast(FP8X4),
                scales=w2_s[:].rearrange("p g n -> p (g n)"),
                in_=w2_g[:].rearrange("p g n k -> p (g n k)"),
            )

        def tail():
            r = H // P - 1
            banks = [ps_h.tile([P, S], F32, name="acc") for vh in range(2)]
            for vh in range(2):
                for d in range(D):
                    g = picks.tile([P, P], F32, name=f"half{d}")
                    part = pos_t[d][:, vh * (P // 16) : (vh + 1) * (P // 16)]
                    nc.vector.tensor_tensor(
                        g[:], h_tiles[r][:].indirect(part), gate_t[:, d, vh * P : vh * P + P], MULT
                    )
                    nc.tensor.matmul(
                        banks[vh][:, 0:P], g[:], ident[:], start=(d == 0), stop=(d == D - 1), is_transpose=True
                    )
            for vh in range(2):
                dst, src = zT[:, vh, r * P : r * P + P], banks[vh][:, 0:P]
                if vh == 0:
                    nc.scalar.activation(dst, src, COPY)
                else:
                    nc.vector.tensor_copy(dst, src)
            res = keep.tile([N, V], F32, name="res")
            for vh in range(2):
                zw = ps_h.tile([P, S], F32, name="acc")
                words = zT[:, vh, 512:1024].bitcast(F32)
                for u in range(2):
                    nc.tensor.transpose(zw[:, u * P : u * P + P], words[:, u::2], ident[:])
                zq = keep.tile([P, P, 4], BF16, name=f"zq_tail{vh}", align_bytes=64)
                dst = zq[:].rearrange("p v k -> p (v k)").bitcast(F32).rearrange("p (v u) -> p v u", u=2)
                src = zw[:, 0 : 2 * P].rearrange("p (u v) -> p v u", u=2)
                if vh == 0:
                    nc.scalar.copy(dst, src)
                else:
                    nc.vector.tensor_copy(dst, src)
                zc = keep.tile([P, P], U32, name=f"zc_tail{vh}", align_bytes=64)
                zs = keep.tile([P, P], U8, name=f"zs_tail{vh}", align_bytes=64)
                nc.vector.quantize_mx(
                    out=zc[:].bitcast(FP8X4), scales=zs[:], in_=zq[:].rearrange("p v k -> p (v k)")
                )
                z_codes[1, vh] = (zc[:], zs[:])
                acc_o = ps_1.tile([N, P], F32, name=f"acc_o{vh}")
                for g in range(GROUPS):
                    zc, zs = z_codes[g, vh]
                    nc.tensor.matmul_mx(
                        out=acc_o[:],
                        lhsT=w2_c[:, g, :].bitcast(FP8X4),
                        lhsT_scale=w2_s[:, g, :],
                        rhs=zc.bitcast(FP8X4),
                        rhs_scale=zs,
                        start=(g == 0),
                        stop=(g == GROUPS - 1),
                    )
                cols = slice(vh * P, vh * P + P)
                if vh == 0:
                    nc.scalar.activation(res[:, cols], acc_o[:], COPY)
                else:
                    nc.vector.tensor_copy(res[:, cols], acc_o[:])
                nc.sync.dma_start(out[:, cols], res[:, cols])

        pick_pairs(0, 0)
        quantise_w1(0)
        pick_pairs(0, 1)
        pick_pairs(1, 0)
        pick_pairs(1, 1)
        project_first()
        quantise_w1(1)
        quantise_w1(2)
        project(1)
        project(2)
        quantise_w1(3)
        aggregate((0, 1))
        project(3)
        weights2()
        quantise_w1(4)
        aggregate((2, 3))
        project(4)
        aggregate((4, 5))
        aggregate((6,))
        second_operand(0)
        tail()
